import numpy as np
import ml_dtypes


def mxq(x, axis, fmt="e4m3"):
    dtype, down = {"e4m3": (ml_dtypes.float8_e4m3fn, 7), "e5m2": (ml_dtypes.float8_e5m2, 14)}[fmt]
    v = np.moveaxis(np.asarray(x, np.float32).astype(ml_dtypes.bfloat16).astype(np.float64), axis, -1)
    blocks = v.reshape(v.shape[:-1] + (-1, 32))
    amax = np.abs(blocks).max(-1, keepdims=True)
    byte = np.maximum(np.where(amax > 0, np.frexp(amax)[1] - 1 + 127, 0) - down, 1)
    scale = np.exp2(byte - 127.0)
    codes = (blocks / scale).astype(np.float32).astype(dtype).astype(np.float64)
    return np.moveaxis((codes * scale).reshape(v.shape), -1, axis)


WIDE = False


def mx_kscale(k):
    if not WIDE:
        return np.ones(k)
    levels = np.array([10, -10, 5, -5, 0])
    if k % 512:
        return np.exp2(np.random.permutation(np.resize(levels, k // 32))).repeat(32)
    a = np.empty((k // 512, 16))
    for p in range(k // 512):
        a[p, :8] = np.random.permutation(np.resize(levels, 8))
        for g in range(8):
            far = levels[np.abs(levels - a[p, g]) >= 10]
            a[p, g + 8] = far[np.random.randint(len(far))]
    return np.exp2(a.ravel()).repeat(32)


def f64(x):
    return np.asarray(x).astype(np.float64)


def striped(idx):
    return np.tile(idx.reshape(-1, 16).T, (8, 1)).astype(np.uint16)


def unstriped(offs):
    return offs[:16].T.reshape(-1).astype(np.int64)


def pack_weight(w):
    k, n = w.shape
    w = f64(np.asarray(w, np.float32).astype(ml_dtypes.bfloat16)).reshape(k // 32, 32, n)
    amax = np.abs(w).max(1)
    byte = np.clip(np.where(amax > 0, np.frexp(amax)[1] - 1 + 127 - 7, 1), 1, 254)
    scaled = (w * np.exp2(127.0 - byte)[:, None, :]).reshape(k, n).astype(np.float32)
    words = np.ascontiguousarray(scaled.reshape(k // 512, 128, 4, n).transpose(0, 1, 3, 2)).astype(ml_dtypes.float8_e4m3fn).view(np.uint8)
    return words, np.ascontiguousarray(byte.astype(np.uint8).reshape(k // 512, 16, n))


def unpack_weight(words, scales):
    g, p, n, _ = words.shape
    vals = np.ascontiguousarray(words).view(ml_dtypes.float8_e4m3fn).astype(np.float64) * np.repeat(np.exp2(scales.astype(np.float64) - 127.0), 8, axis=1)[..., None]
    return vals.transpose(0, 1, 3, 2).reshape(g * 512, n)


K, T, S, H, N = 512, 2048, 512, 512, 128


def setup_inputs():
    n = np.random.standard_normal
    s = mx_kscale(K)[:, None]
    u = mx_kscale(H)
    packed_xT = pack_weight(n((K, T)) * s)
    return {
        "x_words": packed_xT[0],
        "x_scales": packed_xT[1],
        "wc": (n((K, H)) / np.sqrt(K) / s).astype(np.float32),
        "ws": (n((K, H)) / np.sqrt(K) / s).astype(np.float32),
        "unit": (np.random.uniform(0.5, 1.0, (H, 1)) * u[:, None]).astype(np.float32),
        "vc": (n((H, N)) / np.sqrt(2 * H) / u[:, None]).astype(np.float32),
        "vs": (n((H, N)) / np.sqrt(2 * H) / u[:, None]).astype(np.float32),
        "offs": striped(np.random.permutation(T)[:S]),
        "mic": striped(np.random.permutation(T)[:S]),
    }


def reference(x_words, x_scales, wc, ws, unit, vc, vs, offs, mic):
    xq = unpack_weight(x_words, x_scales)[:, unstriped(offs)]
    wcq = mxq(f64(wc), 0, "e4m3")
    ar = wcq.T @ xq
    x_mic = unpack_weight(x_words, x_scales)[:, unstriped(mic)]
    br = wcq.T @ x_mic
    wsq = mxq(f64(ws), 0, "e4m3")
    ai = wsq.T @ xq
    bi = wsq.T @ x_mic
    re = ar * br + ai * bi
    im = ai * br - (ar * bi)
    mag = np.sqrt((re) ** 2 + (im) ** 2 + 0.05)
    zvc = f64(unit) * (re / mag)
    zvs = f64(unit) * (im / mag)
    return mxq(f64(vc), 0, "e4m3").T @ mxq(zvc, 0, "e4m3") + mxq(f64(vs), 0, "e4m3").T @ mxq(zvs, 0, "e4m3")

@@ -1,0 +1,233 @@
+from contextlib import ExitStack
+
+import concourse.mybir as mybir
+from concourse.masks import make_identity
+
+K, T, S, H, N = 512, 2048, 512, 512, 128
+FLOPS = 4 * 2 * K * H * S + 2 * 2 * H * N * S
+
+F32 = mybir.dt.float32
+BF16 = mybir.dt.bfloat16
+I32 = mybir.dt.int32
+U32 = mybir.dt.uint32
+U16 = mybir.dt.uint16
+U8 = mybir.dt.uint8
+FP8X4 = mybir.dt.float8_e4m3fn_x4
+ACT = mybir.ActivationFunctionType
+MULT = mybir.AluOpType.mult
+ADD = mybir.AluOpType.add
+
+P = 128
+PACK = 4
+PAIRS = 128
+BLOCKS = S // PAIRS
+HALF = S // 2
+EPS = 0.05
+
+
+def tile_picked_yphat_phat_p_kernel(
+    tc, x_words, x_scales, wc, ws, unit, vc, vs, offs, mic, out
+):
+    nc = tc.nc
+    with ExitStack() as ctx:
+        keep = ctx.enter_context(tc.tile_pool(name="keep", bufs=1))
+        ring = ctx.enter_context(tc.tile_pool(name="ring", bufs=4))
+        psum = ctx.enter_context(tc.psum_pool(name="psum", bufs=1))
+
+        lists = []
+        for name, src in (("offs", offs), ("mic", mic)):
+            tile = keep.tile([P, S // 16], U16, name="list_" + name)
+            nc.sync.dma_start(tile[:], src)
+            lists.append(tile)
+
+        table_scales = keep.tile([P, T], U8, align_bytes=64)
+        nc.vector.memset(table_scales[:].bitcast(I32), 0)
+        scale_rows = x_scales[0].rearrange("(q r) c -> r q c", r=4)
+        for r in range(4):
+            nc.sync.dma_start(table_scales[r:P:32, :].bitcast(I32), scale_rows[r].bitcast(I32))
+
+        wc_raw = keep.tile([P, PACK, H], F32)
+        nc.sync.dma_start(wc_raw[:], wc.rearrange("(p j) c -> p j c", j=PACK))
+        table_words = keep.tile([P, T], U32, align_bytes=64)
+        nc.sync.dma_start(table_words[:].bitcast(I32), x_words[0].rearrange("p c r -> p (c r)").bitcast(I32))
+        ws_raw = []
+        for half in range(2):
+            tile = keep.tile([P, PACK, H // 2], F32, name="ws_raw", tag="ws_raw_%d" % half)
+            nc.sync.dma_start(tile[:], ws.rearrange("(p j) c -> p j c", j=PACK)[:, :, 256 * half : 256 * (half + 1)])
+            ws_raw.append(tile)
+        v_raw = []
+        for name, src in (("vc", vc), ("vs", vs)):
+            tile = keep.tile([P, PACK, N], F32, name="raw_" + name)
+            nc.sync.dma_start(tile[:], src.rearrange("(p j) c -> p j c", j=PACK))
+            v_raw.append(tile)
+        unit4 = keep.tile([P, PACK], F32)
+        nc.sync.dma_start(unit4[:], unit.rearrange("(p t) o -> p (t o)", t=PACK))
+
+        identity = keep.tile([P, P], F32)
+        make_identity(nc, identity[:])
+        warm = keep.tile([P, 1], F32)
+        nc.scalar.activation(warm[:], identity[:, 0:1], ACT.Abs_reciprocal_sqrt, bias=EPS)
+
+        picked_scales = []
+        for side in range(2):
+            tile = keep.tile([P, S], U8, name="picked_scales_%d" % side, align_bytes=64)
+            nc.vector.tensor_copy(tile[:], table_scales[:].indirect(lists[side][:]))
+            picked_scales.append(tile)
+
+        def interleave(copy, grouped, raw):
+            copy(grouped.rearrange("p (c i) j -> p c j i", i=4), raw.rearrange("p j (c i) -> p c j i", i=4))
+
+        def quantise(grouped, width, name):
+            codes = keep.tile([P, width], U32, name=name + "_codes", align_bytes=64)
+            scales = keep.tile([P, width], U8, name=name + "_scales", align_bytes=64)
+            nc.vector.quantize_mx(
+                out=codes[:].bitcast(FP8X4), scales=scales[:], in_=grouped[:].rearrange("p c j -> p (c j)")
+            )
+            return codes, scales
+
+        wc_grouped = keep.tile([P, H, PACK], BF16, align_bytes=64)
+        interleave(nc.vector.tensor_copy, wc_grouped[:], wc_raw[:])
+        wcq = quantise(wc_grouped, H, "wc")
+
+        picked_words = [[None, None], [None, None]]
+
+        def gather_words(half):
+            for side in range(2):
+                tile = keep.tile([P, HALF], U32, name="picked_words_%d_%d" % (side, half), align_bytes=64)
+                nc.vector.tensor_copy(tile[:], table_words[:].indirect(lists[side][:, 16 * half : 16 * (half + 1)]))
+                picked_words[side][half] = tile
+
+        def spectrum(side, block, wq, tag):
+            bank = psum.tile([P, H], F32, name="spectrum", tag=tag)
+            half, start = divmod(block * PAIRS, HALF)
+            nc.tensor.matmul_mx(
+                out=bank[:],
+                lhsT=picked_words[side][half][:, start : start + PAIRS].bitcast(FP8X4),
+                lhsT_scale=picked_scales[side][:, block * PAIRS : (block + 1) * PAIRS],
+                rhs=wq[0][:].bitcast(FP8X4),
+                rhs_scale=wq[1][:],
+                start=True,
+                stop=True,
+            )
+            return bank[:].rearrange("p (m t) -> p t m", t=PACK)
+
+        def first_side(block, wq, tag, home=None):
+            bank = spectrum(0, block, wq, tag)
+            if home is None:
+                moved = ring.tile([P, PACK, P], F32, name="moved", bufs=8)
+            else:
+                moved = keep.tile([P, PACK, P], F32, name="moved_home", tag=home)
+            nc.scalar.copy(moved[:], bank)
+            return moved
+
+        def product(bank, moved, sign=None):
+            prod = ring.tile([P, PACK, P], F32, name="prod", bufs=16)
+            if sign is None:
+                nc.vector.tensor_tensor(prod[:], bank, moved[:], MULT)
+            else:
+                nc.vector.scalar_tensor_tensor(prod[:], bank, sign, moved[:], MULT, MULT)
+            return prod
+
+        def turn_and_add(first, second, tag):
+            bank = psum.tile([P, PACK, PAIRS], F32, name="cross", tag=tag)
+            for t in range(PACK):
+                nc.tensor.matmul(bank[:, t, :], first[:, t, :], identity[:], start=True, stop=False, is_transpose=True)
+                nc.tensor.matmul(bank[:, t, :], second[:, t, :], identity[:], start=False, stop=True, is_transpose=True)
+            return bank
+
+        def cross(block, ar, ai, br, bi, rr):
+            ir = product(br, ai)
+            ii = product(bi, ai)
+            ri = product(bi, ar, -1.0)
+            re = turn_and_add(rr, ii, banks[block][0])
+            im = turn_and_add(ir, ri, banks[block][1])
+            re2 = ring.tile([P, PACK, PAIRS], F32)
+            im2 = ring.tile([P, PACK, PAIRS], F32)
+            nc.scalar.activation(re2[:], re[:], ACT.Square)
+            nc.scalar.activation(im2[:], im[:], ACT.Square)
+            power = ring.tile([P, PACK, PAIRS], F32)
+            nc.gpsimd.tensor_tensor(power[:], re2[:], im2[:], ADD)
+            inverse = ring.tile([P, PACK, PAIRS], F32)
+            nc.scalar.activation(inverse[:], power[:], ACT.Abs_reciprocal_sqrt, bias=EPS)
+            factor = ring.tile([P, PACK, PAIRS], F32)
+            if block < 2:
+                nc.gpsimd.tensor_tensor(factor[:], inverse[:], unit_rows[:], MULT)
+            else:
+                for t in range(PACK):
+                    nc.scalar.activation(factor[:, t, :], inverse[:, t, :], ACT.Copy, scale=unit4[:, t : t + 1])
+            return re, im, factor
+
+        def finish(block, re, im, factor):
+            z = ring.tile([P, 2, PAIRS, PACK], BF16, align_bytes=64)
+            for part, bank in enumerate((re, im)):
+                nc.vector.tensor_tensor(
+                    z[:, part].rearrange("p (c i) t -> p c t i", i=4),
+                    bank[:].rearrange("p t (c i) -> p c t i", i=4),
+                    factor[:].rearrange("p t (c i) -> p c t i", i=4),
+                    MULT,
+                )
+            z_codes = ring.tile([P, 2 * PAIRS], U32, align_bytes=64)
+            z_scales = ring.tile([P, 2 * PAIRS], U8, align_bytes=64)
+            nc.vector.quantize_mx(
+                out=z_codes[:].bitcast(FP8X4), scales=z_scales[:], in_=z[:].rearrange("p s j t -> p (s j t)")
+            )
+            lags = psum.tile([P, PAIRS], F32, name="lags", tag=banks[block][0])
+            for part in range(2):
+                cols = slice(part * PAIRS, (part + 1) * PAIRS)
+                nc.tensor.matmul_mx(
+                    out=lags[:],
+                    lhsT=vq[0][:, cols].bitcast(FP8X4),
+                    lhsT_scale=vq[1][:, cols],
+                    rhs=z_codes[:, cols].bitcast(FP8X4),
+                    rhs_scale=z_scales[:, cols],
+                    start=(part == 0),
+                    stop=(part == 1),
+                )
+            result = ring.tile([P, PAIRS], F32)
+            nc.scalar.copy(result[:], lags[:])
+            nc.sync.dma_start(out[:, block * PAIRS : (block + 1) * PAIRS], result[:])
+
+        banks = [("b%dr" % block, "b%di" % block) for block in range(BLOCKS)]
+        spare = banks[BLOCKS - 1]
+
+        gather_words(0)
+        gather_words(1)
+        ws_grouped = keep.tile([P, H, PACK], BF16, align_bytes=64)
+        interleave(nc.scalar.copy, ws_grouped[:, 0:256, :], ws_raw[0][:])
+        interleave(nc.vector.tensor_copy, ws_grouped[:, 256:512, :], ws_raw[1][:])
+        wsq = quantise(ws_grouped, H, "ws")
+
+        ar, br, ai, bi, rr = [], [], [], [], []
+        for block in range(3):
+            ar.append(first_side(block, wcq, spare[block % 2], "ws_raw_0" if block == 0 else None))
+            br.append(spectrum(1, block, wcq, banks[block][0]))
+            rr.append(product(br[block], ar[block]))
+        for block in range(3):
+            ai.append(first_side(block, wsq, spare[(block + 1) % 2]))
+            bi.append(spectrum(1, block, wsq, banks[block][1]))
+        ar.append(first_side(3, wcq, spare[0]))
+        ai.append(first_side(3, wsq, spare[1]))
+        br.append(spectrum(1, 3, wcq, banks[3][0]))
+        bi.append(spectrum(1, 3, wsq, banks[3][1]))
+
+        unit_rows = keep.tile([P, PACK, PAIRS], F32)
+        nc.gpsimd.tensor_scalar(unit_rows[:], unit4[:].unsqueeze(2).to_broadcast([P, PACK, PAIRS]), 1.0, 0.0, MULT, ADD)
+        v_grouped = keep.tile([P, 2 * N, PACK], BF16, align_bytes=64)
+        for part in range(2):
+            nc.gpsimd.tensor_scalar(
+                v_grouped[:, part * N : (part + 1) * N, :].rearrange("p (c i) j -> p c j i", i=4),
+                v_raw[part][:].rearrange("p j (c i) -> p c j i", i=4),
+                1.0,
+                0.0,
+                MULT,
+                ADD,
+            )
+
+        pending = []
+        for block in range(BLOCKS):
+            if block == 3:
+                rr.append(product(br[block], ar[block]))
+            pending.append(cross(block, ar[block], ai[block], br[block], bi[block], rr[block]))
+        vq = quantise(v_grouped, 2 * N, "v")
+        for block in range(BLOCKS):
+            finish(block, *pending[block])

@@ -41,7 +41,7 @@ def tile_picked_yphat_phat_p_kernel(
             lists.append(tile)
 
         table_scales = keep.tile([P, T], U8, align_bytes=64)
-        nc.vector.memset(table_scales[:].bitcast(I32), 0)
+        nc.gpsimd.memset(table_scales[:].bitcast(I32), 0)
         scale_rows = x_scales[0].rearrange("(q r) c -> r q c", r=4)
         for r in range(4):
             nc.sync.dma_start(table_scales[r:P:32, :].bitcast(I32), scale_rows[r].bitcast(I32))
@@ -78,7 +78,7 @@ def tile_picked_yphat_phat_p_kernel(
             copy(grouped.rearrange("p (c i) j -> p c j i", i=4), raw.rearrange("p j (c i) -> p c j i", i=4))
 
         def quantise(grouped, width, name):
-            codes = keep.tile([P, width], U32, name=name + "_codes", align_bytes=64)
+            codes = keep.tile([P, width], U32, name=name + "_codes", tag=name + "_codes", align_bytes=64)
             scales = keep.tile([P, width], U8, name=name + "_scales", align_bytes=64)
             nc.vector.quantize_mx(
                 out=codes[:].bitcast(FP8X4), scales=scales[:], in_=grouped[:].rearrange("p c j -> p (c j)")
@@ -120,12 +120,9 @@ def tile_picked_yphat_phat_p_kernel(
             nc.scalar.copy(moved[:], bank)
             return moved
 
-        def product(bank, moved, sign=None):
-            prod = ring.tile([P, PACK, P], F32, name="prod", bufs=16)
-            if sign is None:
-                nc.vector.tensor_tensor(prod[:], bank, moved[:], MULT)
-            else:
-                nc.vector.scalar_tensor_tensor(prod[:], bank, sign, moved[:], MULT, MULT)
+        def product(bank, moved):
+            prod = ring.tile([P, PACK, P], F32, name="prod", bufs=12)
+            nc.vector.tensor_tensor(prod[:], bank, moved[:], MULT)
             return prod
 
         def turn_and_add(first, second, tag):
@@ -136,26 +133,34 @@ def tile_picked_yphat_phat_p_kernel(
             return bank
 
         def cross(block, ar, ai, br, bi, rr):
-            ir = product(br, ai)
+            if block == BLOCKS - 1:
+                ir = keep.tile([P, PACK, P], F32, name="ir", tag="v_codes", align_bytes=64)
+                nc.vector.tensor_tensor(ir[:], br, ai[:], MULT)
+            else:
+                ir = product(br, ai)
             ii = product(bi, ai)
-            ri = product(bi, ar, -1.0)
-            re = turn_and_add(rr, ii, banks[block][0])
-            im = turn_and_add(ir, ri, banks[block][1])
+            ri = keep.tile([P, PACK, P], F32, name="ri", tag="ri_%d" % block)
+            nc.vector.scalar_tensor_tensor(ri[:], bi, -1.0, ar[:], MULT, MULT)
+            re = turn_and_add(rr, ii, banks[block][block // 3])
+            im = turn_and_add(ir, ri, banks[block][1 - block // 3])
             re2 = ring.tile([P, PACK, PAIRS], F32)
             im2 = ring.tile([P, PACK, PAIRS], F32)
             nc.scalar.activation(re2[:], re[:], ACT.Square)
             nc.scalar.activation(im2[:], im[:], ACT.Square)
             power = ring.tile([P, PACK, PAIRS], F32)
             nc.gpsimd.tensor_tensor(power[:], re2[:], im2[:], ADD)
-            inverse = ring.tile([P, PACK, PAIRS], F32)
+            return re, im, power
+
+        def normalise(block, power):
+            inverse = keep.tile([P, PACK, PAIRS], F32, name="inverse", tag="ri_%d" % (block + 1))
             nc.scalar.activation(inverse[:], power[:], ACT.Abs_reciprocal_sqrt, bias=EPS)
             factor = ring.tile([P, PACK, PAIRS], F32)
-            if block < 2:
+            if block == 0:
                 nc.gpsimd.tensor_tensor(factor[:], inverse[:], unit_rows[:], MULT)
             else:
                 for t in range(PACK):
                     nc.scalar.activation(factor[:, t, :], inverse[:, t, :], ACT.Copy, scale=unit4[:, t : t + 1])
-            return re, im, factor
+            return factor
 
         def finish(block, re, im, factor):
             z = ring.tile([P, 2, PAIRS, PACK], BF16, align_bytes=64)
@@ -171,7 +176,7 @@ def tile_picked_yphat_phat_p_kernel(
             nc.vector.quantize_mx(
                 out=z_codes[:].bitcast(FP8X4), scales=z_scales[:], in_=z[:].rearrange("p s j t -> p (s j t)")
             )
-            lags = psum.tile([P, PAIRS], F32, name="lags", tag=banks[block][0])
+            lags = psum.tile([P, PAIRS], F32, name="lags", tag=banks[block][block // 3])
             for part in range(2):
                 cols = slice(part * PAIRS, (part + 1) * PAIRS)
                 nc.tensor.matmul_mx(
@@ -188,31 +193,28 @@ def tile_picked_yphat_phat_p_kernel(
             nc.sync.dma_start(out[:, block * PAIRS : (block + 1) * PAIRS], result[:])
 
         banks = [("b%dr" % block, "b%di" % block) for block in range(BLOCKS)]
-        spare = banks[BLOCKS - 1]
 
         gather_words(0)
         gather_words(1)
-        ws_grouped = keep.tile([P, H, PACK], BF16, align_bytes=64)
+        ws_grouped = keep.tile([P, H, PACK], BF16, align_bytes=64, tag="grouped")
         interleave(nc.scalar.copy, ws_grouped[:, 0:256, :], ws_raw[0][:])
         interleave(nc.vector.tensor_copy, ws_grouped[:, 256:512, :], ws_raw[1][:])
         wsq = quantise(ws_grouped, H, "ws")
 
         ar, br, ai, bi, rr = [], [], [], [], []
         for block in range(3):
-            ar.append(first_side(block, wcq, spare[block % 2], "ws_raw_0" if block == 0 else None))
+            ar.append(first_side(block, wcq, banks[block][1], "ws_raw_0" if block == 0 else None))
             br.append(spectrum(1, block, wcq, banks[block][0]))
             rr.append(product(br[block], ar[block]))
         for block in range(3):
-            ai.append(first_side(block, wsq, spare[(block + 1) % 2]))
+            ai.append(first_side(block, wsq, banks[3][block % 2]))
             bi.append(spectrum(1, block, wsq, banks[block][1]))
-        ar.append(first_side(3, wcq, spare[0]))
-        ai.append(first_side(3, wsq, spare[1]))
-        br.append(spectrum(1, 3, wcq, banks[3][0]))
-        bi.append(spectrum(1, 3, wsq, banks[3][1]))
+        ar.append(first_side(3, wcq, banks[3][1]))
+        ai.append(first_side(3, wsq, banks[3][0]))
+        br.append(spectrum(1, 3, wcq, banks[3][1]))
+        bi.append(spectrum(1, 3, wsq, banks[3][0]))
 
-        unit_rows = keep.tile([P, PACK, PAIRS], F32)
-        nc.gpsimd.tensor_scalar(unit_rows[:], unit4[:].unsqueeze(2).to_broadcast([P, PACK, PAIRS]), 1.0, 0.0, MULT, ADD)
-        v_grouped = keep.tile([P, 2 * N, PACK], BF16, align_bytes=64)
+        v_grouped = keep.tile([P, 2 * N, PACK], BF16, align_bytes=64, tag="grouped")
         for part in range(2):
             nc.gpsimd.tensor_scalar(
                 v_grouped[:, part * N : (part + 1) * N, :].rearrange("p (c i) j -> p c j i", i=4),
@@ -223,11 +225,17 @@ def tile_picked_yphat_phat_p_kernel(
                 ADD,
             )
 
-        pending = []
+        unit_rows = keep.tile([P, PACK, PAIRS], F32)
+        nc.gpsimd.tensor_scalar(unit_rows[:], unit4[:].unsqueeze(2).to_broadcast([P, PACK, PAIRS]), 1.0, 0.0, MULT, ADD)
+
+        pending, factors = [], []
         for block in range(BLOCKS):
             if block == 3:
                 rr.append(product(br[block], ar[block]))
             pending.append(cross(block, ar[block], ai[block], br[block], bi[block], rr[block]))
+            if block > 0:
+                factors.append(normalise(block - 1, pending[block - 1][2]))
+        factors.append(normalise(3, pending[3][2]))
         vq = quantise(v_grouped, 2 * N, "v")
         for block in range(BLOCKS):
-            finish(block, *pending[block])
+            finish(block, pending[block][0], pending[block][1], factors[block])

@@ -75,7 +75,7 @@ def tile_picked_yphat_phat_p_kernel(
             picked_scales.append(tile)
 
         def interleave(copy, grouped, raw):
-            copy(grouped.rearrange("p (c i) j -> p c j i", i=4), raw.rearrange("p j (c i) -> p c j i", i=4))
+            copy(grouped.rearrange("p (c i) j -> p c j i", i=2), raw.rearrange("p j (c i) -> p c j i", i=2))
 
         def quantise(grouped, width, name):
             codes = keep.tile([P, width], U32, name=name + "_codes", tag=name + "_codes", align_bytes=64)
@@ -132,55 +132,67 @@ def tile_picked_yphat_phat_p_kernel(
                 nc.tensor.matmul(bank[:, t, :], second[:, t, :], identity[:], start=False, stop=True, is_transpose=True)
             return bank
 
-        def cross(block, ar, ai, br, bi, rr):
-            if block == BLOCKS - 1:
-                ir = keep.tile([P, PACK, P], F32, name="ir", tag="v_codes", align_bytes=64)
-                nc.vector.tensor_tensor(ir[:], br, ai[:], MULT)
-            else:
-                ir = product(br, ai)
-            ii = product(bi, ai)
-            ri = keep.tile([P, PACK, P], F32, name="ri", tag="ri_%d" % block)
-            nc.vector.scalar_tensor_tensor(ri[:], bi, -1.0, ar[:], MULT, MULT)
-            re = turn_and_add(rr, ii, banks[block][block // 3])
-            im = turn_and_add(ir, ri, banks[block][1 - block // 3])
+        def cross(block):
+            ri = ring.tile([P, PACK, P], F32, name="ri")
+            nc.vector.scalar_tensor_tensor(ri[:], bi[block], -1.0, ar[block][:], MULT, MULT)
+            ir = product(br[block], ai[block])
+            ii = keep.tile([P, PACK, P], F32, name="ii", tag="ri_%d" % block)
+            nc.vector.tensor_tensor(ii[:], bi[block], ai[block][:], MULT)
+            im = turn_and_add(ir, ri, banks[block][0])
+            re = turn_and_add(rr[block], ii, banks[block][1])
+            return re, im
+
+        def pieces(block):
+            width = PAIRS // 2 if block == BLOCKS - 1 else PAIRS
+            return [slice(start, start + width) for start in range(0, PAIRS, width)]
+
+        def powers(block, re, im):
             re2 = ring.tile([P, PACK, PAIRS], F32)
             im2 = ring.tile([P, PACK, PAIRS], F32)
-            nc.scalar.activation(re2[:], re[:], ACT.Square)
             nc.scalar.activation(im2[:], im[:], ACT.Square)
-            power = ring.tile([P, PACK, PAIRS], F32)
-            nc.gpsimd.tensor_tensor(power[:], re2[:], im2[:], ADD)
-            return re, im, power
+            result = []
+            for cols in pieces(block):
+                nc.scalar.activation(re2[:, :, cols], re[:, :, cols], ACT.Square)
+                power = ring.tile([P, PACK, cols.stop - cols.start], F32, name="power", bufs=5)
+                nc.gpsimd.tensor_tensor(power[:], re2[:, :, cols], im2[:, :, cols], ADD)
+                result.append(power)
+            return result
 
-        def normalise(block, power):
-            inverse = keep.tile([P, PACK, PAIRS], F32, name="inverse", tag="ri_%d" % (block + 1))
-            nc.scalar.activation(inverse[:], power[:], ACT.Abs_reciprocal_sqrt, bias=EPS)
-            factor = ring.tile([P, PACK, PAIRS], F32)
-            if block == 0:
-                nc.gpsimd.tensor_tensor(factor[:], inverse[:], unit_rows[:], MULT)
-            else:
-                for t in range(PACK):
-                    nc.scalar.activation(factor[:, t, :], inverse[:, t, :], ACT.Copy, scale=unit4[:, t : t + 1])
-            return factor
+        def normalise(block, power_pieces):
+            result = []
+            for n, power in enumerate(power_pieces):
+                width = power.shape[2]
+                inverse = keep.tile([P, PACK, width], F32, name="inverse", tag="ri_%d" % (block + 1 + n))
+                nc.scalar.activation(inverse[:], power[:], ACT.Abs_reciprocal_sqrt, bias=EPS)
+                factor = ring.tile([P, PACK, width], F32, name="factor", bufs=5)
+                if block == 0:
+                    nc.gpsimd.tensor_tensor(factor[:], inverse[:], unit_rows[:], MULT)
+                else:
+                    for t in range(PACK):
+                        nc.scalar.activation(factor[:, t, :], inverse[:, t, :], ACT.Copy, scale=unit4[:, t : t + 1])
+                result.append(factor)
+            return result
 
-        def finish(block, re, im, factor):
+        def finish(block, re, im, factor_pieces, lags_bank):
             z = ring.tile([P, 2, PAIRS, PACK], BF16, align_bytes=64)
-            for part, bank in enumerate((re, im)):
-                nc.vector.tensor_tensor(
-                    z[:, part].rearrange("p (c i) t -> p c t i", i=4),
-                    bank[:].rearrange("p t (c i) -> p c t i", i=4),
-                    factor[:].rearrange("p t (c i) -> p c t i", i=4),
-                    MULT,
-                )
+            for cols, factor in zip(pieces(block), factor_pieces):
+                for part, bank in enumerate((re, im)):
+                    nc.vector.tensor_tensor(
+                        z[:, part, cols, :].rearrange("p (c i) t -> p c t i", i=2),
+                        bank[:, :, cols].rearrange("p t (c i) -> p c t i", i=2),
+                        factor[:].rearrange("p t (c i) -> p c t i", i=2),
+                        MULT,
+                    )
             z_codes = ring.tile([P, 2 * PAIRS], U32, align_bytes=64)
             z_scales = ring.tile([P, 2 * PAIRS], U8, align_bytes=64)
             nc.vector.quantize_mx(
                 out=z_codes[:].bitcast(FP8X4), scales=z_scales[:], in_=z[:].rearrange("p s j t -> p (s j t)")
             )
-            lags = psum.tile([P, PAIRS], F32, name="lags", tag=banks[block][block // 3])
+            lags = lags_bank(block)
             for part in range(2):
                 cols = slice(part * PAIRS, (part + 1) * PAIRS)
                 nc.tensor.matmul_mx(
-                    out=lags[:],
+                    out=lags,
                     lhsT=vq[0][:, cols].bitcast(FP8X4),
                     lhsT_scale=vq[1][:, cols],
                     rhs=z_codes[:, cols].bitcast(FP8X4),
@@ -188,9 +200,11 @@ def tile_picked_yphat_phat_p_kernel(
                     start=(part == 0),
                     stop=(part == 1),
                 )
-            result = ring.tile([P, PAIRS], F32)
+
+        def store(lags, cols, home):
+            result = keep.tile([P, cols.stop - cols.start], F32, name="result", tag=home)
             nc.scalar.copy(result[:], lags[:])
-            nc.sync.dma_start(out[:, block * PAIRS : (block + 1) * PAIRS], result[:])
+            nc.sync.dma_start(out[:, cols], result[:])
 
         banks = [("b%dr" % block, "b%di" % block) for block in range(BLOCKS)]
 
@@ -205,20 +219,17 @@ def tile_picked_yphat_phat_p_kernel(
         for block in range(3):
             ar.append(first_side(block, wcq, banks[block][1], "ws_raw_0" if block == 0 else None))
             br.append(spectrum(1, block, wcq, banks[block][0]))
-            rr.append(product(br[block], ar[block]))
         for block in range(3):
-            ai.append(first_side(block, wsq, banks[3][block % 2]))
+            ai.append(first_side(block, wsq, banks[3][block % 2], "ai_%d" % block))
             bi.append(spectrum(1, block, wsq, banks[block][1]))
-        ar.append(first_side(3, wcq, banks[3][1]))
-        ai.append(first_side(3, wsq, banks[3][0]))
-        br.append(spectrum(1, 3, wcq, banks[3][1]))
-        bi.append(spectrum(1, 3, wsq, banks[3][0]))
+        for block in range(2):
+            rr.append(product(br[block], ar[block]))
 
         v_grouped = keep.tile([P, 2 * N, PACK], BF16, align_bytes=64, tag="grouped")
         for part in range(2):
             nc.gpsimd.tensor_scalar(
-                v_grouped[:, part * N : (part + 1) * N, :].rearrange("p (c i) j -> p c j i", i=4),
-                v_raw[part][:].rearrange("p j (c i) -> p c j i", i=4),
+                v_grouped[:, part * N : (part + 1) * N, :].rearrange("p (c i) j -> p c j i", i=2),
+                v_raw[part][:].rearrange("p j (c i) -> p c j i", i=2),
                 1.0,
                 0.0,
                 MULT,
@@ -228,14 +239,38 @@ def tile_picked_yphat_phat_p_kernel(
         unit_rows = keep.tile([P, PACK, PAIRS], F32)
         nc.gpsimd.tensor_scalar(unit_rows[:], unit4[:].unsqueeze(2).to_broadcast([P, PACK, PAIRS]), 1.0, 0.0, MULT, ADD)
 
-        pending, factors = [], []
+        crosses, squares, factors = [], [], []
         for block in range(BLOCKS):
-            if block == 3:
+            if block == 2:
                 rr.append(product(br[block], ar[block]))
-            pending.append(cross(block, ar[block], ai[block], br[block], bi[block], rr[block]))
+            if block == 3:
+                last = keep.tile([P, PACK, P], F32, name="rr", tag="v_codes", align_bytes=64)
+                nc.vector.tensor_tensor(last[:], br[block], ar[block][:], MULT)
+                rr.append(last)
+            crosses.append(cross(block))
+            if block == 0:
+                ar.append(first_side(3, wcq, banks[3][1], "ai_0"))
+            if block == 1:
+                ai.append(first_side(3, wsq, banks[3][0], "ai_1"))
+                bi.append(spectrum(1, 3, wsq, banks[3][1]))
+                br.append(spectrum(1, 3, wcq, banks[3][0]))
+            squares.append(powers(block, *crosses[block]))
             if block > 0:
-                factors.append(normalise(block - 1, pending[block - 1][2]))
-        factors.append(normalise(3, pending[3][2]))
+                factors.append(normalise(block - 1, squares[block - 1]))
+        factors.append(normalise(3, squares[3]))
         vq = quantise(v_grouped, 2 * N, "v")
+        held = {}
+
+        def lags_bank(block):
+            if block == 0:
+                held["early"] = psum.tile([P, 3 * PAIRS], F32, name="early", tag=banks[0][0])
+            if block == 3:
+                held["late"] = psum.tile([P, PAIRS], F32, name="late", tag=banks[0][1])
+                return held["late"][:]
+            return held["early"][:, block * PAIRS : (block + 1) * PAIRS]
+
         for block in range(BLOCKS):
-            finish(block, pending[block][0], pending[block][1], factors[block])
+            finish(block, *crosses[block], factors[block], lags_bank)
+            if block == 2:
+                store(held["early"], slice(0, 3 * PAIRS), "ri_5")
+        store(held["late"], slice(3 * PAIRS, S), "ri_4")

@@ -143,18 +143,19 @@ def tile_picked_yphat_phat_p_kernel(
             return re, im
 
         def pieces(block):
-            width = PAIRS // 2 if block == BLOCKS - 1 else PAIRS
+            width = PAIRS
             return [slice(start, start + width) for start in range(0, PAIRS, width)]
 
         def powers(block, re, im):
-            re2 = ring.tile([P, PACK, PAIRS], F32)
-            im2 = ring.tile([P, PACK, PAIRS], F32)
+            re2 = keep.tile([P, PACK, PAIRS], F32, name="re2", tag="re2_%d" % block, align_bytes=64)
+            im2 = keep.tile([P, PACK, PAIRS], F32, name="im2", tag="im2_%d" % block, align_bytes=64)
             nc.scalar.activation(im2[:], im[:], ACT.Square)
             result = []
             for cols in pieces(block):
                 nc.scalar.activation(re2[:, :, cols], re[:, :, cols], ACT.Square)
                 power = ring.tile([P, PACK, cols.stop - cols.start], F32, name="power", bufs=5)
-                nc.gpsimd.tensor_tensor(power[:], re2[:, :, cols], im2[:, :, cols], ADD)
+                adder = nc.vector if block == BLOCKS - 1 else nc.gpsimd
+                adder.tensor_tensor(power[:], re2[:, :, cols], im2[:, :, cols], ADD)
                 result.append(power)
             return result
 
@@ -173,30 +174,35 @@ def tile_picked_yphat_phat_p_kernel(
                 result.append(factor)
             return result
 
-        def finish(block, re, im, factor_pieces, lags_bank):
-            z = ring.tile([P, 2, PAIRS, PACK], BF16, align_bytes=64)
-            for cols, factor in zip(pieces(block), factor_pieces):
-                for part, bank in enumerate((re, im)):
+        def phases(block, z):
+            for cols, factor in zip(pieces(block), factors[block]):
+                for part, bank in enumerate(crosses[block]):
                     nc.vector.tensor_tensor(
-                        z[:, part, cols, :].rearrange("p (c i) t -> p c t i", i=2),
+                        z[:, part * PAIRS + cols.start : part * PAIRS + cols.stop, :].rearrange("p (c i) t -> p c t i", i=2),
                         bank[:, :, cols].rearrange("p t (c i) -> p c t i", i=2),
                         factor[:].rearrange("p t (c i) -> p c t i", i=2),
                         MULT,
                     )
-            z_codes = ring.tile([P, 2 * PAIRS], U32, align_bytes=64)
-            z_scales = ring.tile([P, 2 * PAIRS], U8, align_bytes=64)
+
+        def quantise_pair(grouped, home):
+            width = grouped.shape[1]
+            codes = keep.tile([P, width], U32, name="late_codes", tag=home, align_bytes=64)
+            scales = keep.tile([P, width], U8, name="late_scales", tag="scales_" + home, align_bytes=64)
             nc.vector.quantize_mx(
-                out=z_codes[:].bitcast(FP8X4), scales=z_scales[:], in_=z[:].rearrange("p s j t -> p (s j t)")
+                out=codes[:].bitcast(FP8X4), scales=scales[:], in_=grouped[:].rearrange("p c j -> p (c j)")
             )
-            lags = lags_bank(block)
+            return codes, scales
+
+        def lags(bank, vq, zq, start):
             for part in range(2):
-                cols = slice(part * PAIRS, (part + 1) * PAIRS)
+                cols = slice(start + part * PAIRS, start + (part + 1) * PAIRS)
+                rows = slice(part * N, (part + 1) * N)
                 nc.tensor.matmul_mx(
-                    out=lags,
-                    lhsT=vq[0][:, cols].bitcast(FP8X4),
-                    lhsT_scale=vq[1][:, cols],
-                    rhs=z_codes[:, cols].bitcast(FP8X4),
-                    rhs_scale=z_scales[:, cols],
+                    out=bank,
+                    lhsT=vq[0][:, rows].bitcast(FP8X4),
+                    lhsT_scale=vq[1][:, rows],
+                    rhs=zq[0][:, cols].bitcast(FP8X4),
+                    rhs_scale=zq[1][:, cols],
                     start=(part == 0),
                     stop=(part == 1),
                 )
@@ -225,7 +231,10 @@ def tile_picked_yphat_phat_p_kernel(
         for block in range(2):
             rr.append(product(br[block], ar[block]))
 
-        v_grouped = keep.tile([P, 2 * N, PACK], BF16, align_bytes=64, tag="grouped")
+        unit_rows = keep.tile([P, PACK, PAIRS], F32)
+        nc.gpsimd.tensor_scalar(unit_rows[:], unit4[:].unsqueeze(2).to_broadcast([P, PACK, PAIRS]), 1.0, 0.0, MULT, ADD)
+
+        v_grouped = keep.tile([P, 2 * N + 2 * PAIRS, PACK], BF16, align_bytes=64, tag="grouped")
         for part in range(2):
             nc.gpsimd.tensor_scalar(
                 v_grouped[:, part * N : (part + 1) * N, :].rearrange("p (c i) j -> p c j i", i=2),
@@ -236,17 +245,10 @@ def tile_picked_yphat_phat_p_kernel(
                 ADD,
             )
 
-        unit_rows = keep.tile([P, PACK, PAIRS], F32)
-        nc.gpsimd.tensor_scalar(unit_rows[:], unit4[:].unsqueeze(2).to_broadcast([P, PACK, PAIRS]), 1.0, 0.0, MULT, ADD)
-
         crosses, squares, factors = [], [], []
         for block in range(BLOCKS):
-            if block == 2:
+            if block >= 2:
                 rr.append(product(br[block], ar[block]))
-            if block == 3:
-                last = keep.tile([P, PACK, P], F32, name="rr", tag="v_codes", align_bytes=64)
-                nc.vector.tensor_tensor(last[:], br[block], ar[block][:], MULT)
-                rr.append(last)
             crosses.append(cross(block))
             if block == 0:
                 ar.append(first_side(3, wcq, banks[3][1], "ai_0"))
@@ -258,19 +260,20 @@ def tile_picked_yphat_phat_p_kernel(
             if block > 0:
                 factors.append(normalise(block - 1, squares[block - 1]))
         factors.append(normalise(3, squares[3]))
-        vq = quantise(v_grouped, 2 * N, "v")
-        held = {}
-
-        def lags_bank(block):
-            if block == 0:
-                held["early"] = psum.tile([P, 3 * PAIRS], F32, name="early", tag=banks[0][0])
-            if block == 3:
-                held["late"] = psum.tile([P, PAIRS], F32, name="late", tag=banks[0][1])
-                return held["late"][:]
-            return held["early"][:, block * PAIRS : (block + 1) * PAIRS]
-
-        for block in range(BLOCKS):
-            finish(block, *crosses[block], factors[block], lags_bank)
-            if block == 2:
-                store(held["early"], slice(0, 3 * PAIRS), "ri_5")
-        store(held["late"], slice(3 * PAIRS, S), "ri_4")
+        phases(0, v_grouped[:, 2 * N :, :])
+        middle = keep.tile([P, 4 * PAIRS, PACK], BF16, align_bytes=64)
+        phases(1, middle[:, : 2 * PAIRS, :])
+        phases(2, middle[:, 2 * PAIRS :, :])
+        vq = quantise_pair(v_grouped, "re2_3")
+        middle_q = quantise_pair(middle, "im2_3")
+        early = psum.tile([P, 3 * PAIRS], F32, tag=banks[0][0])
+        lags(early[:, 0:PAIRS], vq, vq, 2 * N)
+        lags(early[:, PAIRS : 2 * PAIRS], vq, middle_q, 0)
+        lags(early[:, 2 * PAIRS :], vq, middle_q, 2 * PAIRS)
+        store(early, slice(0, 3 * PAIRS), "ri_4")
+        last = keep.tile([P, 2 * PAIRS, PACK], BF16, align_bytes=64)
+        phases(3, last[:])
+        last_q = quantise_pair(last, "re2_2")
+        late = psum.tile([P, PAIRS], F32, tag=banks[0][1])
+        lags(late[:], vq, last_q, 0)
+        store(late, slice(3 * PAIRS, S), "ri_0")

from contextlib import ExitStack

import concourse.mybir as mybir
from concourse.masks import make_identity

K, T, S, H, N = 512, 2048, 512, 512, 128
FLOPS = 4 * 2 * K * H * S + 2 * 2 * H * N * S

F32 = mybir.dt.float32
BF16 = mybir.dt.bfloat16
I32 = mybir.dt.int32
U32 = mybir.dt.uint32
U16 = mybir.dt.uint16
U8 = mybir.dt.uint8
FP8X4 = mybir.dt.float8_e4m3fn_x4
ACT = mybir.ActivationFunctionType
MULT = mybir.AluOpType.mult
ADD = mybir.AluOpType.add

P = 128
PACK = 4
PAIRS = 128
BLOCKS = S // PAIRS
HALF = S // 2
EPS = 0.05


def tile_picked_yphat_phat_p_kernel(
    tc, x_words, x_scales, wc, ws, unit, vc, vs, offs, mic, out
):
    nc = tc.nc
    with ExitStack() as ctx:
        keep = ctx.enter_context(tc.tile_pool(name="keep", bufs=1))
        ring = ctx.enter_context(tc.tile_pool(name="ring", bufs=4))
        psum = ctx.enter_context(tc.psum_pool(name="psum", bufs=1))

        lists = []
        for name, src in (("offs", offs), ("mic", mic)):
            tile = keep.tile([P, S // 16], U16, name="list_" + name)
            nc.sync.dma_start(tile[:], src)
            lists.append(tile)

        table_scales = keep.tile([P, T], U8, align_bytes=64)
        nc.gpsimd.memset(table_scales[:].bitcast(I32), 0)
        scale_rows = x_scales[0].rearrange("(q r) c -> r q c", r=4)
        for r in range(4):
            nc.sync.dma_start(table_scales[r:P:32, :].bitcast(I32), scale_rows[r].bitcast(I32))

        wc_raw = keep.tile([P, PACK, H], F32)
        nc.sync.dma_start(wc_raw[:], wc.rearrange("(p j) c -> p j c", j=PACK))
        table_words = keep.tile([P, T], U32, align_bytes=64)
        nc.sync.dma_start(table_words[:].bitcast(I32), x_words[0].rearrange("p c r -> p (c r)").bitcast(I32))
        ws_raw = []
        for half in range(2):
            tile = keep.tile([P, PACK, H // 2], F32, name="ws_raw", tag="ws_raw_%d" % half)
            nc.sync.dma_start(tile[:], ws.rearrange("(p j) c -> p j c", j=PACK)[:, :, 256 * half : 256 * (half + 1)])
            ws_raw.append(tile)
        v_raw = []
        for name, src in (("vc", vc), ("vs", vs)):
            tile = keep.tile([P, PACK, N], F32, name="raw_" + name)
            nc.sync.dma_start(tile[:], src.rearrange("(p j) c -> p j c", j=PACK))
            v_raw.append(tile)
        unit4 = keep.tile([P, PACK], F32)
        nc.sync.dma_start(unit4[:], unit.rearrange("(p t) o -> p (t o)", t=PACK))

        identity = keep.tile([P, P], F32)
        make_identity(nc, identity[:])
        warm = keep.tile([P, 1], F32)
        nc.scalar.activation(warm[:], identity[:, 0:1], ACT.Abs_reciprocal_sqrt, bias=EPS)

        picked_scales = []
        for side in range(2):
            tile = keep.tile([P, S], U8, name="picked_scales_%d" % side, align_bytes=64)
            nc.vector.tensor_copy(tile[:], table_scales[:].indirect(lists[side][:]))
            picked_scales.append(tile)

        def interleave(copy, grouped, raw):
            copy(grouped.rearrange("p (c i) j -> p c j i", i=2), raw.rearrange("p j (c i) -> p c j i", i=2))

        def quantise(grouped, width, name):
            codes = keep.tile([P, width], U32, name=name + "_codes", tag=name + "_codes", align_bytes=64)
            scales = keep.tile([P, width], U8, name=name + "_scales", align_bytes=64)
            nc.vector.quantize_mx(
                out=codes[:].bitcast(FP8X4), scales=scales[:], in_=grouped[:].rearrange("p c j -> p (c j)")
            )
            return codes, scales

        wc_grouped = keep.tile([P, H, PACK], BF16, align_bytes=64)
        interleave(nc.vector.tensor_copy, wc_grouped[:], wc_raw[:])
        wcq = quantise(wc_grouped, H, "wc")

        picked_words = [[None, None], [None, None]]

        def gather_words(half):
            for side in range(2):
                tile = keep.tile([P, HALF], U32, name="picked_words_%d_%d" % (side, half), align_bytes=64)
                nc.vector.tensor_copy(tile[:], table_words[:].indirect(lists[side][:, 16 * half : 16 * (half + 1)]))
                picked_words[side][half] = tile

        def spectrum(side, block, wq, tag):
            bank = psum.tile([P, H], F32, name="spectrum", tag=tag)
            half, start = divmod(block * PAIRS, HALF)
            nc.tensor.matmul_mx(
                out=bank[:],
                lhsT=picked_words[side][half][:, start : start + PAIRS].bitcast(FP8X4),
                lhsT_scale=picked_scales[side][:, block * PAIRS : (block + 1) * PAIRS],
                rhs=wq[0][:].bitcast(FP8X4),
                rhs_scale=wq[1][:],
                start=True,
                stop=True,
            )
            return bank[:].rearrange("p (m t) -> p t m", t=PACK)

        def first_side(block, wq, tag, home=None):
            bank = spectrum(0, block, wq, tag)
            if home is None:
                moved = ring.tile([P, PACK, P], F32, name="moved", bufs=8)
            else:
                moved = keep.tile([P, PACK, P], F32, name="moved_home", tag=home)
            nc.scalar.copy(moved[:], bank)
            return moved

        def product(bank, moved):
            prod = ring.tile([P, PACK, P], F32, name="prod", bufs=12)
            nc.vector.tensor_tensor(prod[:], bank, moved[:], MULT)
            return prod

        def turn_and_add(first, second, tag):
            bank = psum.tile([P, PACK, PAIRS], F32, name="cross", tag=tag)
            for t in range(PACK):
                nc.tensor.matmul(bank[:, t, :], first[:, t, :], identity[:], start=True, stop=False, is_transpose=True)
                nc.tensor.matmul(bank[:, t, :], second[:, t, :], identity[:], start=False, stop=True, is_transpose=True)
            return bank

        def cross(block):
            ri = ring.tile([P, PACK, P], F32, name="ri")
            nc.vector.scalar_tensor_tensor(ri[:], bi[block], -1.0, ar[block][:], MULT, MULT)
            ir = product(br[block], ai[block])
            ii = keep.tile([P, PACK, P], F32, name="ii", tag="ri_%d" % block)
            nc.vector.tensor_tensor(ii[:], bi[block], ai[block][:], MULT)
            im = turn_and_add(ir, ri, banks[block][0])
            re = turn_and_add(rr[block], ii, banks[block][1])
            return re, im

        def pieces(block):
            width = PAIRS
            return [slice(start, start + width) for start in range(0, PAIRS, width)]

        def powers(block, re, im):
            re2 = keep.tile([P, PACK, PAIRS], F32, name="re2", tag="re2_%d" % block, align_bytes=64)
            im2 = keep.tile([P, PACK, PAIRS], F32, name="im2", tag="im2_%d" % block, align_bytes=64)
            nc.scalar.activation(im2[:], im[:], ACT.Square)
            result = []
            for cols in pieces(block):
                nc.scalar.activation(re2[:, :, cols], re[:, :, cols], ACT.Square)
                power = ring.tile([P, PACK, cols.stop - cols.start], F32, name="power", bufs=5)
                adder = nc.vector if block == BLOCKS - 1 else nc.gpsimd
                adder.tensor_tensor(power[:], re2[:, :, cols], im2[:, :, cols], ADD)
                result.append(power)
            return result

        def normalise(block, power_pieces):
            result = []
            for n, power in enumerate(power_pieces):
                width = power.shape[2]
                inverse = keep.tile([P, PACK, width], F32, name="inverse", tag="ri_%d" % (block + 1 + n))
                nc.scalar.activation(inverse[:], power[:], ACT.Abs_reciprocal_sqrt, bias=EPS)
                factor = ring.tile([P, PACK, width], F32, name="factor", bufs=5)
                if block == 0:
                    nc.gpsimd.tensor_tensor(factor[:], inverse[:], unit_rows[:], MULT)
                else:
                    for t in range(PACK):
                        nc.scalar.activation(factor[:, t, :], inverse[:, t, :], ACT.Copy, scale=unit4[:, t : t + 1])
                result.append(factor)
            return result

        def phases(block, z):
            for cols, factor in zip(pieces(block), factors[block]):
                for part, bank in enumerate(crosses[block]):
                    nc.vector.tensor_tensor(
                        z[:, part * PAIRS + cols.start : part * PAIRS + cols.stop, :].rearrange("p (c i) t -> p c t i", i=2),
                        bank[:, :, cols].rearrange("p t (c i) -> p c t i", i=2),
                        factor[:].rearrange("p t (c i) -> p c t i", i=2),
                        MULT,
                    )

        def quantise_pair(grouped, home):
            width = grouped.shape[1]
            codes = keep.tile([P, width], U32, name="late_codes", tag=home, align_bytes=64)
            scales = keep.tile([P, width], U8, name="late_scales", tag="scales_" + home, align_bytes=64)
            nc.vector.quantize_mx(
                out=codes[:].bitcast(FP8X4), scales=scales[:], in_=grouped[:].rearrange("p c j -> p (c j)")
            )
            return codes, scales

        def lags(bank, vq, zq, start):
            for part in range(2):
                cols = slice(start + part * PAIRS, start + (part + 1) * PAIRS)
                rows = slice(part * N, (part + 1) * N)
                nc.tensor.matmul_mx(
                    out=bank,
                    lhsT=vq[0][:, rows].bitcast(FP8X4),
                    lhsT_scale=vq[1][:, rows],
                    rhs=zq[0][:, cols].bitcast(FP8X4),
                    rhs_scale=zq[1][:, cols],
                    start=(part == 0),
                    stop=(part == 1),
                )

        def store(lags, cols, home):
            result = keep.tile([P, cols.stop - cols.start], F32, name="result", tag=home)
            nc.scalar.copy(result[:], lags[:])
            nc.sync.dma_start(out[:, cols], result[:])

        banks = [("b%dr" % block, "b%di" % block) for block in range(BLOCKS)]

        gather_words(0)
        gather_words(1)
        ws_grouped = keep.tile([P, H, PACK], BF16, align_bytes=64, tag="grouped")
        interleave(nc.scalar.copy, ws_grouped[:, 0:256, :], ws_raw[0][:])
        interleave(nc.vector.tensor_copy, ws_grouped[:, 256:512, :], ws_raw[1][:])
        wsq = quantise(ws_grouped, H, "ws")

        ar, br, ai, bi, rr = [], [], [], [], []
        for block in range(3):
            ar.append(first_side(block, wcq, banks[block][1], "ws_raw_0" if block == 0 else None))
            br.append(spectrum(1, block, wcq, banks[block][0]))
        for block in range(3):
            ai.append(first_side(block, wsq, banks[3][block % 2], "ai_%d" % block))
            bi.append(spectrum(1, block, wsq, banks[block][1]))
        for block in range(2):
            rr.append(product(br[block], ar[block]))

        unit_rows = keep.tile([P, PACK, PAIRS], F32)
        nc.gpsimd.tensor_scalar(unit_rows[:], unit4[:].unsqueeze(2).to_broadcast([P, PACK, PAIRS]), 1.0, 0.0, MULT, ADD)

        v_grouped = keep.tile([P, 2 * N + 2 * PAIRS, PACK], BF16, align_bytes=64, tag="grouped")
        for part in range(2):
            nc.gpsimd.tensor_scalar(
                v_grouped[:, part * N : (part + 1) * N, :].rearrange("p (c i) j -> p c j i", i=2),
                v_raw[part][:].rearrange("p j (c i) -> p c j i", i=2),
                1.0,
                0.0,
                MULT,
                ADD,
            )

        crosses, squares, factors = [], [], []
        for block in range(BLOCKS):
            if block >= 2:
                rr.append(product(br[block], ar[block]))
            crosses.append(cross(block))
            if block == 0:
                ar.append(first_side(3, wcq, banks[3][1], "ai_0"))
            if block == 1:
                ai.append(first_side(3, wsq, banks[3][0], "ai_1"))
                bi.append(spectrum(1, 3, wsq, banks[3][1]))
                br.append(spectrum(1, 3, wcq, banks[3][0]))
            squares.append(powers(block, *crosses[block]))
            if block > 0:
                factors.append(normalise(block - 1, squares[block - 1]))
        factors.append(normalise(3, squares[3]))
        phases(0, v_grouped[:, 2 * N :, :])
        middle = keep.tile([P, 4 * PAIRS, PACK], BF16, align_bytes=64)
        phases(1, middle[:, : 2 * PAIRS, :])
        phases(2, middle[:, 2 * PAIRS :, :])
        vq = quantise_pair(v_grouped, "re2_3")
        middle_q = quantise_pair(middle, "im2_3")
        early = psum.tile([P, 3 * PAIRS], F32, tag=banks[0][0])
        lags(early[:, 0:PAIRS], vq, vq, 2 * N)
        lags(early[:, PAIRS : 2 * PAIRS], vq, middle_q, 0)
        lags(early[:, 2 * PAIRS :], vq, middle_q, 2 * PAIRS)
        store(early, slice(0, 3 * PAIRS), "ri_4")
        last = keep.tile([P, 2 * PAIRS, PACK], BF16, align_bytes=64)
        phases(3, last[:])
        last_q = quantise_pair(last, "re2_2")
        late = psum.tile([P, PAIRS], F32, tag=banks[0][1])
        lags(late[:], vq, last_q, 0)
        store(late, slice(3 * PAIRS, S), "ri_0")
